import numpy as np
import ml_dtypes


def mxq(x, axis, fmt="e4m3"):
    dtype, down = {"e4m3": (ml_dtypes.float8_e4m3fn, 7), "e5m2": (ml_dtypes.float8_e5m2, 14)}[fmt]
    v = np.moveaxis(np.asarray(x, np.float32).astype(ml_dtypes.bfloat16).astype(np.float64), axis, -1)
    blocks = v.reshape(v.shape[:-1] + (-1, 32))
    amax = np.abs(blocks).max(-1, keepdims=True)
    byte = np.maximum(np.where(amax > 0, np.frexp(amax)[1] - 1 + 127, 0) - down, 1)
    scale = np.exp2(byte - 127.0)
    codes = (blocks / scale).astype(np.float32).astype(dtype).astype(np.float64)
    return np.moveaxis((codes * scale).reshape(v.shape), -1, axis)


WIDE = False


def mx_kscale(k):
    if not WIDE:
        return np.ones(k)
    levels = np.array([30, -30])
    if k % 512:
        return np.exp2(np.random.permutation(np.resize(levels, k // 32))).repeat(32)
    a = np.empty((k // 512, 16))
    for p in range(k // 512):
        a[p, :8] = np.random.permutation(np.resize(levels, 8))
        for g in range(8):
            far = levels[np.abs(levels - a[p, g]) >= 10]
            a[p, g + 8] = far[np.random.randint(len(far))]
    return np.exp2(a.ravel()).repeat(32)


def f64(x):
    return np.asarray(x).astype(np.float64)


def striped(idx):
    return np.tile(np.asarray(idx).reshape(-1, 16).T, (8, 1)).astype(np.uint16)


def unstriped(offs):
    return offs[:16].T.reshape(-1).astype(np.int64)


E2M1 = np.array([0.0, 0.5, 1.0, 1.5, 2.0, 3.0, 4.0, 6.0, -0.0, -0.5, -1.0, -1.5, -2.0, -3.0, -4.0, -6.0])


def pack_weight(w, fmt):
    k, n = w.shape
    w = f64(np.asarray(w, np.float32).astype(ml_dtypes.bfloat16)).reshape(k // 32, 32, n)
    amax = np.abs(w).max(1)
    if fmt == "e4m3":
        byte = np.frexp(amax)[1] - 1 + 127 - 7
    else:
        mant, ex = np.frexp(amax / 6.0)
        byte = np.where(mant > 0.5, ex, ex - 1) + 127
    byte = np.clip(np.where(amax > 0, byte, 1), 1, 254)
    scaled = (w * np.exp2(127.0 - byte)[:, None, :]).reshape(k, n).astype(np.float32)
    by_word = np.ascontiguousarray(scaled.reshape(k // 512, 128, 4, n).transpose(0, 1, 3, 2))
    if fmt == "e4m3":
        words = by_word.astype(ml_dtypes.float8_e4m3fn).view(np.uint8)
    else:
        c = by_word.astype(ml_dtypes.float4_e2m1fn).view(np.uint8) & 0xF
        words = (c[..., 0::2] | (c[..., 1::2] << 4)).reshape(k // 512, 128, 2 * n)
    return np.ascontiguousarray(words), np.ascontiguousarray(byte.astype(np.uint8).reshape(k // 512, 16, n))


def unpack_weight(words, scales, fmt):
    g, _, n = scales.shape
    words = np.ascontiguousarray(words).reshape(g, 128, n, -1)
    if fmt == "e4m3":
        vals = words.view(ml_dtypes.float8_e4m3fn).astype(np.float64)
    else:
        nib = np.empty((g, 128, n, 4), np.uint8)
        nib[..., 0::2] = words & 0xF
        nib[..., 1::2] = words >> 4
        vals = E2M1[nib]
    vals = vals * np.repeat(np.exp2(scales.astype(np.float64) - 127.0), 8, axis=1)[..., None]
    return vals.transpose(0, 1, 3, 2).reshape(g * 512, n)


def sigmoid(v):
    return 1.0 / (1.0 + np.exp(-v))


def sgn(shape):
    return np.random.uniform(0.5, 2.0, shape) * np.where(np.random.standard_normal(shape) < 0, -1.0, 1.0)


K, T, J, R, I, O, N, S, E = 512, 1024, 256, 512, 256, 128, 256, 1024, 512


def setup_inputs():
    n = np.random.standard_normal
    idx = np.random.permutation(T)[:J]
    idx2 = np.random.permutation(J)[:I]
    idx3 = np.random.permutation(J)[:I]
    idx4 = np.random.permutation(S)[:N]
    idx5 = np.random.permutation(E)[:O]
    idx6 = np.random.permutation(E)[:O]
    fk = mx_kscale(K)
    fr = mx_kscale(R)
    xtp = pack_weight(n((K, T)) / fk[:, None], "e2m1")
    wp = pack_weight(n((K, R)) * 1 / np.sqrt(K) * fk[:, None], "e4m3")
    vsp = pack_weight(n((R, S)) * 1 / np.sqrt(R) / fr[:, None], "e2m1")
    return {
        "xt_words": xtp[0],
        "xt_scales": xtp[1],
        "w_words": wp[0],
        "w_scales": wp[1],
        "sa": (sgn((R, 1)) * fr[:, None]).astype(np.float32),
        "sg": (sgn((R, 1))).astype(np.float32),
        "bg": (np.random.uniform(-2.0, 2.0, (R, 1))).astype(np.float32),
        "vs_words": vsp[0],
        "vs_scales": vsp[1],
        "offs": striped(idx),
        "offs2": striped(idx2),
        "offs3": striped(idx3),
        "offs4": striped(idx4),
        "offs5": striped(idx5),
        "offs6": striped(idx6),
    }


def reference(xt_words, xt_scales, w_words, w_scales, sa, sg, bg, vs_words, vs_scales, offs, offs2, offs3, offs4, offs5, offs6):
    idx = unstriped(offs)
    idx2 = unstriped(offs2)
    idx3 = unstriped(offs3)
    idx4 = unstriped(offs4)
    idx5 = unstriped(offs5)
    idx6 = unstriped(offs6)
    xtu = unpack_weight(xt_words, xt_scales, "e2m1")
    wu = unpack_weight(w_words, w_scales, "e4m3")
    vsu = unpack_weight(vs_words, vs_scales, "e2m1")
    xtidxg = xtu[:, idx]
    a = wu.T @ xtidxg
    h1 = a[:, idx2] * f64(sa) * sigmoid(a[:, idx3] * f64(sg) + f64(bg))
    hid = h1.reshape(R, O, I // O).max(axis=2)
    vsidx4g = vsu[:, idx4]
    hidq = mxq(hid, 0, "e5m2")
    p = vsidx4g.T @ hidq
    pa = np.zeros((N, E))
    pa[:, idx5] = p
    pb = np.zeros((N, E))
    pb[:, idx6] = p
    y = pa + pb
    return y

@@ -1,0 +1,182 @@
+from contextlib import ExitStack
+
+import concourse.mybir as mybir
+
+F32 = mybir.dt.float32
+BF16 = mybir.dt.bfloat16
+I32 = mybir.dt.int32
+U32 = mybir.dt.uint32
+U16 = mybir.dt.uint16
+U8 = mybir.dt.uint8
+E4M3 = mybir.dt.float8_e4m3fn_x4
+E5M2 = mybir.dt.float8_e5m2_x4
+E2M1 = mybir.dt.float4_e2m1fn_x4
+ACT = mybir.ActivationFunctionType
+ALU = mybir.AluOpType
+
+P = 128
+K, T, J, R, I, O, N, S, E = 512, 1024, 256, 512, 256, 128, 256, 1024, 512
+PACK = 4
+FLOPS = 2 * K * R * J + 2 * R * N * O
+
+
+def tile_list_gatedpool_solo_store_pagetwice_kernel(
+    tc, xt_words, xt_scales, w_words, w_scales, sa, sg, bg, vs_words, vs_scales,
+    offs, offs2, offs3, offs4, offs5, offs6, out,
+):
+    nc = tc.nc
+    with ExitStack() as ctx:
+        keep = ctx.enter_context(tc.tile_pool(name="keep", bufs=1))
+        ring = ctx.enter_context(tc.tile_pool(name="ring", bufs=2))
+        psum = ctx.enter_context(tc.psum_pool(name="psum", bufs=1))
+
+        def sb(name, shape, dtype, tag=None):
+            return keep.tile(shape, dtype, name=name, tag=tag or name, align_bytes=64)
+
+        def load_list(name, src):
+            tile = sb(name, list(src.shape), U16)
+            nc.sync.dma_start(tile[:], src)
+            return tile
+
+        def load_scale_rows(queue, plane, src):
+            rows = src[0].bitcast(I32)
+            for q in range(4):
+                queue.dma_start(plane[32 * q : 32 * q + 4, :].bitcast(I32), rows[4 * q : 4 * q + 4, :])
+
+        def load_per_row(name, src):
+            tile = sb(name, [P, PACK], F32)
+            nc.sync.dma_start(tile[:], src.rearrange("(p t) o -> p (t o)", t=PACK))
+            return tile
+
+        x_plane = sb("x_plane", [P, T], U8)
+        w_plane = sb("w_plane", [P, R], U8)
+        v_plane = sb("v_plane", [P, S], U8)
+        nc.vector.memset(x_plane[:].bitcast(I32), 0)
+        nc.vector.memset(w_plane[:].bitcast(I32), 0)
+        nc.vector.memset(v_plane[:].bitcast(I32), 0)
+
+        w_stage = sb("w_stage", [4, 4, R // 4], I32)
+        nc.sync.dma_start(w_stage[:], w_scales[0].bitcast(I32).rearrange("(q r) c -> r q c", r=4))
+        tok_list = load_list("tok_list", offs)
+        x_words = sb("x_words", [P, T], U16)
+        nc.sync.dma_start(x_words[:].bitcast(I32), xt_words[0].bitcast(I32))
+        load_scale_rows(nc.sync, x_plane, xt_scales)
+        w_raw = sb("w_raw", [P, R], U32)
+        nc.sync.dma_start(w_raw[:].bitcast(I32), w_words[0].rearrange("p n t -> p (n t)").bitcast(I32))
+        pick_list = load_list("pick_list", offs2)
+        weight = load_per_row("weight", sa)
+        gate_list = load_list("gate_list", offs3)
+        slope = load_per_row("slope", sg)
+        offset = load_per_row("offset", bg)
+        store_list = load_list("store_list", offs4)
+        v_words = sb("v_words", [P, S], U16)
+        nc.sync.dma_start(v_words[:].bitcast(I32), vs_words[0].bitcast(I32))
+        load_scale_rows(nc.sync, v_plane, vs_scales)
+        page_lists = [load_list("page_list_a", offs5), load_list("page_list_b", offs6)]
+
+        pages = [[sb("page_0_%d" % l, [P, E], F32) for l in range(2)]]
+        for l in range(2):
+            nc.vector.memset(pages[0][l][:], 0.0)
+
+        for q in range(4):
+            nc.vector.tensor_copy(w_plane[32 * q : 32 * q + 4, :].bitcast(I32), w_stage[:, q, :])
+        w_codes = sb("w_codes", [P, PACK, P], U32)
+        w_sc = sb("w_sc", [P, PACK, P], U8)
+        w_raw_mt = w_raw[:].rearrange("p (m t) -> p m t", t=PACK)
+        w_plane_mt = w_plane[:].rearrange("p (m t) -> p m t", t=PACK)
+        nc.vector.tensor_copy(w_sc[:, 0, :], w_plane_mt[:, :, 0])
+        xg_sc = sb("xg_sc", [P, J], U8)
+        xg = sb("xg", [P, J], U16)
+        nc.vector.tensor_copy(xg[:], x_words[:].indirect(tok_list[:]))
+        for u in range(2):
+            nc.vector.tensor_copy(xg_sc[:, u * P : (u + 1) * P], x_plane[:].indirect(tok_list[:, u * 8 : (u + 1) * 8]))
+        nc.scalar.copy(w_codes[:, 0, :], w_raw_mt[:, :, 0])
+        nc.scalar.copy(w_codes[:, 1:, :].rearrange("p t m -> p m t"), w_raw_mt[:, :, 1:])
+        nc.vector.tensor_copy(w_sc[:, 1:, :].rearrange("p t m -> p m t"), w_plane_mt[:, :, 1:])
+
+        a_rows = []
+        for t in range(PACK):
+            a_t = sb("a_%d" % t, [P, 2 * J], F32)
+            parts = 2 if t == 0 else 1
+            for u in range(parts):
+                cols = slice(u * J // parts, (u + 1) * J // parts)
+                acc = psum.tile([P, J // parts], F32, name="acc_a%d_%d" % (t, u))
+                nc.tensor.matmul_mx(
+                    acc[:], lhsT=w_codes[:, t, :].bitcast(E4M3), lhsT_scale=w_sc[:, t, :],
+                    rhs=xg[:, cols].bitcast(E2M1), rhs_scale=xg_sc[:, cols], start=True, stop=True,
+                )
+                if t == 0:
+                    nc.scalar.copy(a_t[:, cols], acc[:])
+                else:
+                    nc.vector.tensor_copy(a_t[:, cols], acc[:])
+            a_rows.append(a_t)
+
+        pages.append([sb("page_1_0", [P, E], F32, tag="x_words"), sb("page_1_1", [P, E], F32, tag="w_raw")])
+        for l in range(2):
+            nc.gpsimd.memset(pages[1][l][:], 0.0)
+        hid_rows = sb("hid_rows", [P, PACK - 1, O], BF16)
+        vg = sb("vg", [P, N], U16)
+        vg_sc = sb("vg_sc", [P, N], U8)
+        hid = sb("hid", [P, O, PACK], BF16)
+        hq = sb("hq", [P, O], U32)
+        hq_sc = sb("hq_sc", [P, O], U8)
+        for t in range(PACK):
+            last = t == PACK - 1
+            gate = ring.tile([P, I], F32, name="gate")
+            pick = ring.tile([P, I], F32, name="pick")
+            h1 = sb("h1_%d" % t, [P, O, 2], F32)
+            nc.scalar.activation(
+                out=pick[:], in_=a_rows[t][:].indirect(pick_list[:]), func=ACT.Copy, scale=weight[:, t : t + 1],
+            )
+            parts = 2 if last else 1
+            spans = [slice(u * O // parts, (u + 1) * O // parts) for u in range(parts)]
+            for pools in spans:
+                picks = slice(2 * pools.start, 2 * pools.stop)
+                nc.scalar.activation(
+                    out=gate[:, picks], in_=a_rows[t][:].indirect(gate_list[:, picks.start // 16 : picks.stop // 16]),
+                    func=ACT.Sigmoid, bias=offset[:, t : t + 1], scale=slope[:, t : t + 1],
+                )
+                nc.vector.tensor_tensor(
+                    h1[:, pools, :].rearrange("p o two -> p (o two)"), pick[:, picks], gate[:, picks], ALU.mult
+                )
+            if t == 0:
+                nc.vector.tensor_copy(vg[:], v_words[:].indirect(store_list[:]))
+            if t == 1:
+                nc.vector.tensor_copy(vg_sc[:], v_plane[:].indirect(store_list[:]))
+            for pools in spans:
+                dst = hid[:, pools, t] if last else hid_rows[:, t, :]
+                nc.vector.tensor_tensor(dst, h1[:, pools, 0], h1[:, pools, 1], ALU.max)
+            if t == PACK - 2:
+                nc.vector.tensor_copy(hid[:, :, : PACK - 1], hid_rows[:].rearrange("p t o -> p o t"))
+            if last:
+                for pools in spans:
+                    nc.vector.quantize_mx(
+                        out=hq[:, pools].bitcast(E5M2), scales=hq_sc[:, pools],
+                        in_=hid[:, pools, :].rearrange("p o t -> p (o t)"),
+                    )
+
+        ps = []
+        for h in range(N // P):
+            acc = psum.tile([P, O], F32, name="acc_p%d" % h)
+            cols = slice(h * P, (h + 1) * P)
+            nc.tensor.matmul_mx(
+                acc[:], lhsT=vg[:, cols].bitcast(E2M1), lhsT_scale=vg_sc[:, cols],
+                rhs=hq[:].bitcast(E5M2), rhs_scale=hq_sc[:], start=True, stop=True,
+            )
+            p_h = sb("p_%d" % h, [P, O], F32)
+            if h == 0:
+                nc.vector.tensor_copy(p_h[:], acc[:])
+            else:
+                nc.scalar.copy(p_h[:], acc[:])
+            ps.append(p_h)
+        for h in range(N // P):
+            nc.vector.tensor_copy(pages[h][0][:].indirect(page_lists[0][:]), ps[h][:])
+            nc.scalar.activation(out=pages[h][1][:].indirect(page_lists[1][:]), in_=ps[h][:], func=ACT.Copy)
+        for h in range(N // P):
+            res = sb("res_%d" % h, [P, E], F32)
+            parts = 2 if h == N // P - 1 else 1
+            for u in range(parts):
+                cols = slice(u * E // parts, (u + 1) * E // parts)
+                nc.vector.tensor_tensor(res[:, cols], pages[h][0][:, cols], pages[h][1][:, cols], ALU.add)
+                queue = nc.scalar if u == 1 else nc.sync
+                queue.dma_start(out[h * P : (h + 1) * P, cols], res[:, cols])

@@ -63,6 +63,10 @@ def tile_list_gatedpool_solo_store_pagetwice_kernel(
         load_scale_rows(nc.sync, x_plane, xt_scales)
         w_raw = sb("w_raw", [P, R], U32)
         nc.sync.dma_start(w_raw[:].bitcast(I32), w_words[0].rearrange("p n t -> p (n t)").bitcast(I32))
+        warm_in = sb("warm_in", [P, 1], F32)
+        warm_out = sb("warm_out", [P, 1], F32)
+        nc.gpsimd.memset(warm_in[:], 0.0)
+        nc.scalar.activation(out=warm_out[:], in_=warm_in[:], func=ACT.Sigmoid)
         pick_list = load_list("pick_list", offs2)
         weight = load_per_row("weight", sa)
         gate_list = load_list("gate_list", offs3)

@@ -27,7 +27,6 @@ def tile_list_gatedpool_solo_store_pagetwice_kernel(
     nc = tc.nc
     with ExitStack() as ctx:
         keep = ctx.enter_context(tc.tile_pool(name="keep", bufs=1))
-        ring = ctx.enter_context(tc.tile_pool(name="ring", bufs=2))
         psum = ctx.enter_context(tc.psum_pool(name="psum", bufs=1))
 
         def sb(name, shape, dtype, tag=None):
@@ -68,10 +67,10 @@ def tile_list_gatedpool_solo_store_pagetwice_kernel(
         nc.gpsimd.memset(warm_in[:], 0.0)
         nc.scalar.activation(out=warm_out[:], in_=warm_in[:], func=ACT.Sigmoid)
         pick_list = load_list("pick_list", offs2)
-        weight = load_per_row("weight", sa)
         gate_list = load_list("gate_list", offs3)
         slope = load_per_row("slope", sg)
         offset = load_per_row("offset", bg)
+        weight = load_per_row("weight", sa)
         store_list = load_list("store_list", offs4)
         v_words = sb("v_words", [P, S], U16)
         nc.sync.dma_start(v_words[:].bitcast(I32), vs_words[0].bitcast(I32))
@@ -115,22 +114,17 @@ def tile_list_gatedpool_solo_store_pagetwice_kernel(
                     nc.vector.tensor_copy(a_t[:, cols], acc[:])
             a_rows.append(a_t)
 
-        pages.append([sb("page_1_0", [P, E], F32, tag="x_words"), sb("page_1_1", [P, E], F32, tag="w_raw")])
-        for l in range(2):
-            nc.gpsimd.memset(pages[1][l][:], 0.0)
         hid_rows = sb("hid_rows", [P, PACK - 1, O], BF16)
-        vg = sb("vg", [P, N], U16)
-        vg_sc = sb("vg_sc", [P, N], U8)
         hid = sb("hid", [P, O, PACK], BF16)
         hq = sb("hq", [P, O], U32)
         hq_sc = sb("hq_sc", [P, O], U8)
         for t in range(PACK):
             last = t == PACK - 1
-            gate = ring.tile([P, I], F32, name="gate")
-            pick = ring.tile([P, I], F32, name="pick")
+            looked = sb("looked_%d" % t, [P, 2, I], F32, tag="a_%d" % (t - 2) if t >= 2 else None)
+            pick, gate = looked[:, 0, :], looked[:, 1, :]
             h1 = sb("h1_%d" % t, [P, O, 2], F32)
             nc.scalar.activation(
-                out=pick[:], in_=a_rows[t][:].indirect(pick_list[:]), func=ACT.Copy, scale=weight[:, t : t + 1],
+                out=pick, in_=a_rows[t][:].indirect(pick_list[:]), func=ACT.Copy, scale=weight[:, t : t + 1],
             )
             parts = 2 if last else 1
             spans = [slice(u * O // parts, (u + 1) * O // parts) for u in range(parts)]
@@ -144,8 +138,10 @@ def tile_list_gatedpool_solo_store_pagetwice_kernel(
                     h1[:, pools, :].rearrange("p o two -> p (o two)"), pick[:, picks], gate[:, picks], ALU.mult
                 )
             if t == 0:
+                vg = sb("vg", [P, N], U16)
                 nc.vector.tensor_copy(vg[:], v_words[:].indirect(store_list[:]))
             if t == 1:
+                vg_sc = sb("vg_sc", [P, N], U8)
                 nc.vector.tensor_copy(vg_sc[:], v_plane[:].indirect(store_list[:]))
             for pools in spans:
                 dst = hid[:, pools, t] if last else hid_rows[:, t, :]
@@ -159,6 +155,9 @@ def tile_list_gatedpool_solo_store_pagetwice_kernel(
                         in_=hid[:, pools, :].rearrange("p o t -> p (o t)"),
                     )
 
+        pages.append([sb("page_1_%d" % l, [P, E], F32, tag="h1_%d" % l) for l in range(2)])
+        for l in range(2):
+            nc.gpsimd.memset(pages[1][l][:], 0.0)
         ps = []
         for h in range(N // P):
             acc = psum.tile([P, O], F32, name="acc_p%d" % h)

@@ -177,7 +177,7 @@ def tile_list_gatedpool_solo_store_pagetwice_kernel(
             nc.scalar.activation(out=pages[h][1][:].indirect(page_lists[1][:]), in_=ps[h][:], func=ACT.Copy)
         for h in range(N // P):
             res = sb("res_%d" % h, [P, E], F32)
-            parts = 2 if h == N // P - 1 else 1
+            parts = 2
             for u in range(parts):
                 cols = slice(u * E // parts, (u + 1) * E // parts)
                 nc.vector.tensor_tensor(res[:, cols], pages[h][0][:, cols], pages[h][1][:, cols], ALU.add)

from contextlib import ExitStack

import concourse.mybir as mybir

F32 = mybir.dt.float32
BF16 = mybir.dt.bfloat16
I32 = mybir.dt.int32
U32 = mybir.dt.uint32
U16 = mybir.dt.uint16
U8 = mybir.dt.uint8
E4M3 = mybir.dt.float8_e4m3fn_x4
E5M2 = mybir.dt.float8_e5m2_x4
E2M1 = mybir.dt.float4_e2m1fn_x4
ACT = mybir.ActivationFunctionType
ALU = mybir.AluOpType

P = 128
K, T, J, R, I, O, N, S, E = 512, 1024, 256, 512, 256, 128, 256, 1024, 512
PACK = 4
FLOPS = 2 * K * R * J + 2 * R * N * O


def tile_list_gatedpool_solo_store_pagetwice_kernel(
    tc, xt_words, xt_scales, w_words, w_scales, sa, sg, bg, vs_words, vs_scales,
    offs, offs2, offs3, offs4, offs5, offs6, out,
):
    nc = tc.nc
    with ExitStack() as ctx:
        keep = ctx.enter_context(tc.tile_pool(name="keep", bufs=1))
        psum = ctx.enter_context(tc.psum_pool(name="psum", bufs=1))

        def sb(name, shape, dtype, tag=None):
            return keep.tile(shape, dtype, name=name, tag=tag or name, align_bytes=64)

        def load_list(name, src):
            tile = sb(name, list(src.shape), U16)
            nc.sync.dma_start(tile[:], src)
            return tile

        def load_scale_rows(queue, plane, src):
            rows = src[0].bitcast(I32)
            for q in range(4):
                queue.dma_start(plane[32 * q : 32 * q + 4, :].bitcast(I32), rows[4 * q : 4 * q + 4, :])

        def load_per_row(name, src):
            tile = sb(name, [P, PACK], F32)
            nc.sync.dma_start(tile[:], src.rearrange("(p t) o -> p (t o)", t=PACK))
            return tile

        x_plane = sb("x_plane", [P, T], U8)
        w_plane = sb("w_plane", [P, R], U8)
        v_plane = sb("v_plane", [P, S], U8)
        nc.vector.memset(x_plane[:].bitcast(I32), 0)
        nc.vector.memset(w_plane[:].bitcast(I32), 0)
        nc.vector.memset(v_plane[:].bitcast(I32), 0)

        w_stage = sb("w_stage", [4, 4, R // 4], I32)
        nc.sync.dma_start(w_stage[:], w_scales[0].bitcast(I32).rearrange("(q r) c -> r q c", r=4))
        tok_list = load_list("tok_list", offs)
        x_words = sb("x_words", [P, T], U16)
        nc.sync.dma_start(x_words[:].bitcast(I32), xt_words[0].bitcast(I32))
        load_scale_rows(nc.sync, x_plane, xt_scales)
        w_raw = sb("w_raw", [P, R], U32)
        nc.sync.dma_start(w_raw[:].bitcast(I32), w_words[0].rearrange("p n t -> p (n t)").bitcast(I32))
        warm_in = sb("warm_in", [P, 1], F32)
        warm_out = sb("warm_out", [P, 1], F32)
        nc.gpsimd.memset(warm_in[:], 0.0)
        nc.scalar.activation(out=warm_out[:], in_=warm_in[:], func=ACT.Sigmoid)
        pick_list = load_list("pick_list", offs2)
        gate_list = load_list("gate_list", offs3)
        slope = load_per_row("slope", sg)
        offset = load_per_row("offset", bg)
        weight = load_per_row("weight", sa)
        store_list = load_list("store_list", offs4)
        v_words = sb("v_words", [P, S], U16)
        nc.sync.dma_start(v_words[:].bitcast(I32), vs_words[0].bitcast(I32))
        load_scale_rows(nc.sync, v_plane, vs_scales)
        page_lists = [load_list("page_list_a", offs5), load_list("page_list_b", offs6)]

        pages = [[sb("page_0_%d" % l, [P, E], F32) for l in range(2)]]
        for l in range(2):
            nc.vector.memset(pages[0][l][:], 0.0)

        for q in range(4):
            nc.vector.tensor_copy(w_plane[32 * q : 32 * q + 4, :].bitcast(I32), w_stage[:, q, :])
        w_codes = sb("w_codes", [P, PACK, P], U32)
        w_sc = sb("w_sc", [P, PACK, P], U8)
        w_raw_mt = w_raw[:].rearrange("p (m t) -> p m t", t=PACK)
        w_plane_mt = w_plane[:].rearrange("p (m t) -> p m t", t=PACK)
        nc.vector.tensor_copy(w_sc[:, 0, :], w_plane_mt[:, :, 0])
        xg_sc = sb("xg_sc", [P, J], U8)
        xg = sb("xg", [P, J], U16)
        nc.vector.tensor_copy(xg[:], x_words[:].indirect(tok_list[:]))
        for u in range(2):
            nc.vector.tensor_copy(xg_sc[:, u * P : (u + 1) * P], x_plane[:].indirect(tok_list[:, u * 8 : (u + 1) * 8]))
        nc.scalar.copy(w_codes[:, 0, :], w_raw_mt[:, :, 0])
        nc.scalar.copy(w_codes[:, 1:, :].rearrange("p t m -> p m t"), w_raw_mt[:, :, 1:])
        nc.vector.tensor_copy(w_sc[:, 1:, :].rearrange("p t m -> p m t"), w_plane_mt[:, :, 1:])

        a_rows = []
        for t in range(PACK):
            a_t = sb("a_%d" % t, [P, 2 * J], F32)
            parts = 2 if t == 0 else 1
            for u in range(parts):
                cols = slice(u * J // parts, (u + 1) * J // parts)
                acc = psum.tile([P, J // parts], F32, name="acc_a%d_%d" % (t, u))
                nc.tensor.matmul_mx(
                    acc[:], lhsT=w_codes[:, t, :].bitcast(E4M3), lhsT_scale=w_sc[:, t, :],
                    rhs=xg[:, cols].bitcast(E2M1), rhs_scale=xg_sc[:, cols], start=True, stop=True,
                )
                if t == 0:
                    nc.scalar.copy(a_t[:, cols], acc[:])
                else:
                    nc.vector.tensor_copy(a_t[:, cols], acc[:])
            a_rows.append(a_t)

        hid_rows = sb("hid_rows", [P, PACK - 1, O], BF16)
        hid = sb("hid", [P, O, PACK], BF16)
        hq = sb("hq", [P, O], U32)
        hq_sc = sb("hq_sc", [P, O], U8)
        for t in range(PACK):
            last = t == PACK - 1
            looked = sb("looked_%d" % t, [P, 2, I], F32, tag="a_%d" % (t - 2) if t >= 2 else None)
            pick, gate = looked[:, 0, :], looked[:, 1, :]
            h1 = sb("h1_%d" % t, [P, O, 2], F32)
            nc.scalar.activation(
                out=pick, in_=a_rows[t][:].indirect(pick_list[:]), func=ACT.Copy, scale=weight[:, t : t + 1],
            )
            parts = 2 if last else 1
            spans = [slice(u * O // parts, (u + 1) * O // parts) for u in range(parts)]
            for pools in spans:
                picks = slice(2 * pools.start, 2 * pools.stop)
                nc.scalar.activation(
                    out=gate[:, picks], in_=a_rows[t][:].indirect(gate_list[:, picks.start // 16 : picks.stop // 16]),
                    func=ACT.Sigmoid, bias=offset[:, t : t + 1], scale=slope[:, t : t + 1],
                )
                nc.vector.tensor_tensor(
                    h1[:, pools, :].rearrange("p o two -> p (o two)"), pick[:, picks], gate[:, picks], ALU.mult
                )
            if t == 0:
                vg = sb("vg", [P, N], U16)
                nc.vector.tensor_copy(vg[:], v_words[:].indirect(store_list[:]))
            if t == 1:
                vg_sc = sb("vg_sc", [P, N], U8)
                nc.vector.tensor_copy(vg_sc[:], v_plane[:].indirect(store_list[:]))
            for pools in spans:
                dst = hid[:, pools, t] if last else hid_rows[:, t, :]
                nc.vector.tensor_tensor(dst, h1[:, pools, 0], h1[:, pools, 1], ALU.max)
            if t == PACK - 2:
                nc.vector.tensor_copy(hid[:, :, : PACK - 1], hid_rows[:].rearrange("p t o -> p o t"))
            if last:
                for pools in spans:
                    nc.vector.quantize_mx(
                        out=hq[:, pools].bitcast(E5M2), scales=hq_sc[:, pools],
                        in_=hid[:, pools, :].rearrange("p o t -> p (o t)"),
                    )

        pages.append([sb("page_1_%d" % l, [P, E], F32, tag="h1_%d" % l) for l in range(2)])
        for l in range(2):
            nc.gpsimd.memset(pages[1][l][:], 0.0)
        ps = []
        for h in range(N // P):
            acc = psum.tile([P, O], F32, name="acc_p%d" % h)
            cols = slice(h * P, (h + 1) * P)
            nc.tensor.matmul_mx(
                acc[:], lhsT=vg[:, cols].bitcast(E2M1), lhsT_scale=vg_sc[:, cols],
                rhs=hq[:].bitcast(E5M2), rhs_scale=hq_sc[:], start=True, stop=True,
            )
            p_h = sb("p_%d" % h, [P, O], F32)
            if h == 0:
                nc.vector.tensor_copy(p_h[:], acc[:])
            else:
                nc.scalar.copy(p_h[:], acc[:])
            ps.append(p_h)
        for h in range(N // P):
            nc.vector.tensor_copy(pages[h][0][:].indirect(page_lists[0][:]), ps[h][:])
            nc.scalar.activation(out=pages[h][1][:].indirect(page_lists[1][:]), in_=ps[h][:], func=ACT.Copy)
        for h in range(N // P):
            res = sb("res_%d" % h, [P, E], F32)
            parts = 2
            for u in range(parts):
                cols = slice(u * E // parts, (u + 1) * E // parts)
                nc.vector.tensor_tensor(res[:, cols], pages[h][0][:, cols], pages[h][1][:, cols], ALU.add)
                queue = nc.scalar if u == 1 else nc.sync
                queue.dma_start(out[h * P : (h + 1) * P, cols], res[:, cols])
